import numpy as np
import ml_dtypes


def mxq(x, axis, fmt="e4m3"):
    dtype, down = {"e4m3": (ml_dtypes.float8_e4m3fn, 7), "e5m2": (ml_dtypes.float8_e5m2, 14)}[fmt]
    v = np.moveaxis(np.asarray(x, np.float32).astype(ml_dtypes.bfloat16).astype(np.float64), axis, -1)
    blocks = v.reshape(v.shape[:-1] + (-1, 32))
    amax = np.abs(blocks).max(-1, keepdims=True)
    byte = np.maximum(np.where(amax > 0, np.frexp(amax)[1] - 1 + 127, 0) - down, 1)
    scale = np.exp2(byte - 127.0)
    codes = (blocks / scale).astype(np.float32).astype(dtype).astype(np.float64)
    return np.moveaxis((codes * scale).reshape(v.shape), -1, axis)


WIDE = False


def mx_kscale(k):
    if not WIDE:
        return np.ones(k)
    levels = np.array([10, -10, 5, -5, 0])
    if k % 512:
        return np.exp2(np.random.permutation(np.resize(levels, k // 32))).repeat(32)
    a = np.empty((k // 512, 16))
    for p in range(k // 512):
        a[p, :8] = np.random.permutation(np.resize(levels, 8))
        for g in range(8):
            far = levels[np.abs(levels - a[p, g]) >= 10]
            a[p, g + 8] = far[np.random.randint(len(far))]
    return np.exp2(a.ravel()).repeat(32)


def f64(x):
    return np.asarray(x).astype(np.float64)


def striped(idx):
    return np.tile(np.asarray(idx).reshape(-1, 16).T, (8, 1)).astype(np.uint16)


def unstriped(offs):
    return offs[:16].T.reshape(-1).astype(np.int64)


E2M1 = np.array([0.0, 0.5, 1.0, 1.5, 2.0, 3.0, 4.0, 6.0, -0.0, -0.5, -1.0, -1.5, -2.0, -3.0, -4.0, -6.0])


def pack_weight(w, fmt):
    k, n = w.shape
    w = f64(np.asarray(w, np.float32).astype(ml_dtypes.bfloat16)).reshape(k // 32, 32, n)
    amax = np.abs(w).max(1)
    if fmt == "e4m3":
        byte = np.frexp(amax)[1] - 1 + 127 - 7
    else:
        mant, ex = np.frexp(amax / 6.0)
        byte = np.where(mant > 0.5, ex, ex - 1) + 127
    byte = np.clip(np.where(amax > 0, byte, 1), 1, 254)
    scaled = (w * np.exp2(127.0 - byte)[:, None, :]).reshape(k, n).astype(np.float32)
    by_word = np.ascontiguousarray(scaled.reshape(k // 512, 128, 4, n).transpose(0, 1, 3, 2))
    if fmt == "e4m3":
        words = by_word.astype(ml_dtypes.float8_e4m3fn).view(np.uint8)
    else:
        c = by_word.astype(ml_dtypes.float4_e2m1fn).view(np.uint8) & 0xF
        words = (c[..., 0::2] | (c[..., 1::2] << 4)).reshape(k // 512, 128, 2 * n)
    return np.ascontiguousarray(words), np.ascontiguousarray(byte.astype(np.uint8).reshape(k // 512, 16, n))


def unpack_weight(words, scales, fmt):
    g, _, n = scales.shape
    words = np.ascontiguousarray(words).reshape(g, 128, n, -1)
    if fmt == "e4m3":
        vals = words.view(ml_dtypes.float8_e4m3fn).astype(np.float64)
    else:
        nib = np.empty((g, 128, n, 4), np.uint8)
        nib[..., 0::2] = words & 0xF
        nib[..., 1::2] = words >> 4
        vals = E2M1[nib]
    vals = vals * np.repeat(np.exp2(scales.astype(np.float64) - 127.0), 8, axis=1)[..., None]
    return vals.transpose(0, 1, 3, 2).reshape(g * 512, n)


def bf(x):
    return np.asarray(x, np.float32).astype(ml_dtypes.bfloat16)


def planes(Y):
    r, m = Y.shape
    b = f64(bf(Y)).reshape(r // 32, 32, m)
    amax = np.abs(b).max(1)
    byte = np.clip(np.where(amax > 0, np.frexp(amax)[1] - 1 + 127 - 7, 1), 1, 254)
    codes = (b * np.exp2(127.0 - byte)[:, None, :]).reshape(r, m).astype(np.float32).astype(ml_dtypes.float8_e4m3fn).view(np.uint8)
    words = codes.reshape(r // 512, 128, 4, m).transpose(0, 1, 3, 2)
    return np.ascontiguousarray(words), np.ascontiguousarray(byte.astype(np.uint8).reshape(r // 512, 16, m))


D, T, I, J, U, M = 512, 2048, 512, 512, 1024, 1024


def setup_inputs():
    n = np.random.standard_normal
    idx = np.random.permutation(T)[:I]
    idx2 = np.random.permutation(U)[:J]
    idx3 = np.random.permutation(U)[:J]
    idx4 = np.random.permutation(M)[:J]
    fd = mx_kscale(D)
    keysp = pack_weight(n((D, T)) / fd[:, None], "e2m1")
    return {
        "keys_words": keysp[0],
        "keys_scales": keysp[1],
        "notes": (n((D, U)) * 1.0 / np.sqrt(D) * fd[:, None]).astype(np.float32),
        "old": (1.0 * n((I, M))).astype(np.float32),
        "fade": (np.random.uniform(0.3, 0.9, (I, 1))).astype(np.float32),
        "offs": striped(idx),
        "offs2": striped(idx2),
        "offs3": striped(idx3),
        "offs4": striped(idx4),
    }


def reference(keys_words, keys_scales, notes, old, fade, offs, offs2, offs3, offs4):
    idx = unstriped(offs)
    idx2 = unstriped(offs2)
    idx3 = unstriped(offs3)
    idx4 = unstriped(offs4)
    keysu = unpack_weight(keys_words, keys_scales, "e2m1")
    keysidxg = keysu[:, idx]
    notesq = mxq(f64(notes), 0, "e4m3")
    g1 = keysidxg.T @ notesq
    g0 = g1[:, idx2] * g1[:, idx3]
    gf = np.zeros((I, M))
    gf[:, idx4] = g0
    y = f64(old) * f64(fade) + gf
    words, scales = planes(y)
    return y, words, scales

@@ -1,0 +1,213 @@
+from contextlib import ExitStack
+
+import concourse.mybir as mybir
+
+D, T, I, J, U, M = 512, 2048, 512, 512, 1024, 1024
+FLOPS = 2 * D * I * U
+
+F32 = mybir.dt.float32
+BF16 = mybir.dt.bfloat16
+I32 = mybir.dt.int32
+U32 = mybir.dt.uint32
+U16 = mybir.dt.uint16
+U8 = mybir.dt.uint8
+FP8X4 = mybir.dt.float8_e4m3fn_x4
+FP4X4 = mybir.dt.float4_e2m1fn_x4
+MULT = mybir.AluOpType.mult
+ADD = mybir.AluOpType.add
+COPY = mybir.ActivationFunctionType.Copy
+
+P = 128
+PACK = 4
+CHUNK = 256
+HALF = 512
+LIST_COLS = J // 16
+
+
+def interleave(engine_copy, dst, src):
+    engine_copy(
+        dst.rearrange("p (c i) t -> p c t i", i=4),
+        src.rearrange("p t (c i) -> p c t i", i=4),
+    )
+
+
+def tile_attend_tab_lookedtimes_keep_pl_kernel(
+    tc, keys_words, keys_scales, notes, old, fade, offs, offs2, offs3, offs4, out_0, out_1, out_2
+):
+    nc = tc.nc
+
+    def on_vector(dst, src):
+        nc.vector.tensor_copy(dst, src)
+
+    def on_scalar(dst, src):
+        nc.scalar.activation(dst, src, COPY)
+
+    with ExitStack() as ctx:
+        lists = ctx.enter_context(tc.tile_pool(name="lists", bufs=1))
+        keep = ctx.enter_context(tc.tile_pool(name="keep", bufs=1))
+        psum = ctx.enter_context(tc.psum_pool(name="psum", bufs=1))
+
+        def tile(shape, dtype, name):
+            return keep.tile(shape, dtype, name=name, align_bytes=64)
+
+        pool_scales = tile([P, T], U8, "pool_scales")
+        nc.gpsimd.memset(pool_scales[:].bitcast(I32), 0)
+
+        pool_words = tile([P, T], U16, "pool_words")
+        nc.sync.dma_start(pool_words[:].bitcast(I32), keys_words[0].bitcast(I32))
+        token_list = lists.tile([P, LIST_COLS], U16, name="token_list")
+        nc.sync.dma_start(token_list[:], offs)
+        for q in range(4):
+            nc.sync.dma_start(
+                pool_scales[32 * q : 32 * q + 4, :].bitcast(I32),
+                keys_scales[0, 4 * q : 4 * q + 4, :].bitcast(I32),
+            )
+        notes_rows = notes.rearrange("(p t) u -> p t u", t=PACK)
+        notes_raw = []
+        for c in range(U // CHUNK):
+            raw = tile([P, PACK, CHUNK], F32, "notes_raw%d" % c)
+            nc.sync.dma_start(raw[:], notes_rows[:, :, c * CHUNK : (c + 1) * CHUNK])
+            notes_raw.append(raw)
+        first_list = lists.tile([P, LIST_COLS], U16, name="first_list")
+        nc.sync.dma_start(first_list[:], offs2)
+        second_list = lists.tile([P, LIST_COLS], U16, name="second_list")
+        nc.sync.dma_start(second_list[:], offs3)
+        place_list = lists.tile([P, LIST_COLS], U16, name="place_list")
+        nc.sync.dma_start(place_list[:], offs4)
+        fades = tile([P, PACK], F32, "fades")
+        nc.sync.dma_start(fades[:], fade.rearrange("(p t) one -> p (t one)", t=PACK))
+        old_rows = old.rearrange("(p t) m -> p t m", t=PACK)
+        olds = []
+        for t in range(PACK):
+            before = tile([P, M], F32, "old%d" % t)
+            nc.sync.dma_start(before[:], old_rows[:, t, :])
+            olds.append(before)
+
+        placed = [tile([P, M], F32, "placed%d" % t) for t in range(PACK)]
+        for t in range(PACK):
+            nc.vector.memset(placed[t][:], 0.0)
+
+        picked_words = tile([P, I], U16, "picked_words")
+        nc.vector.tensor_copy(picked_words[:], pool_words[:].indirect(token_list[:]))
+        key_words = tile([P, PACK, P], U16, "key_words")
+        nc.vector.tensor_copy(key_words[:], picked_words[:].rearrange("p (s t) -> p t s", t=PACK))
+        key_scales = tile([P, PACK, P], U8, "key_scales")
+        nc.vector.tensor_copy(key_scales[:].rearrange("p t s -> p s t"), pool_scales[:].indirect(token_list[:]))
+
+        note_codes = [tile([P, HALF], U32, "note_codes%d" % h) for h in range(2)]
+        note_scales = [tile([P, HALF], U8, "note_scales%d" % h) for h in range(2)]
+        wide = [tile([P, U], F32, "wide%d" % t) for t in range(PACK)]
+        banks = {}
+
+        def quantise_notes(c, engine_copy):
+            grouped = tile([P, CHUNK, PACK], BF16, "notes_grouped%d" % (c % 2))
+            interleave(engine_copy, grouped[:], notes_raw[c][:])
+            cols = slice((c % 2) * CHUNK, (c % 2 + 1) * CHUNK)
+            nc.vector.quantize_mx(
+                out=note_codes[c // 2][:, cols].bitcast(FP8X4),
+                scales=note_scales[c // 2][:, cols],
+                in_=grouped[:].rearrange("p c t -> p (c t)"),
+            )
+
+        def multiply(h):
+            for t in range(PACK):
+                banks[t, h] = psum.tile([P, HALF], F32, name="bank%d_%d" % (t, h))
+                nc.tensor.matmul_mx(
+                    out=banks[t, h][:],
+                    lhsT=key_words[:, t, :].bitcast(U8).bitcast(FP4X4),
+                    lhsT_scale=key_scales[:, t, :],
+                    rhs=note_codes[h][:].bitcast(FP8X4),
+                    rhs_scale=note_scales[h][:],
+                    start=True,
+                    stop=True,
+                )
+
+        def leave_bank(t, h, engine_copy):
+            engine_copy(wide[t][:, h * HALF : (h + 1) * HALF], banks[t, h][:])
+
+        quantise_notes(0, on_scalar)
+        quantise_notes(1, on_scalar)
+        multiply(0)
+        quantise_notes(2, on_scalar)
+        quantise_notes(3, on_vector)
+        multiply(1)
+
+        firsts = [tile([P, J], F32, "first%d" % t) for t in range(PACK)]
+        seconds = [tile([P, J], F32, "second%d" % t) for t in range(PACK)]
+        result = [tile([P, PACK, HALF], F32, "result%d" % h) for h in range(2)]
+        out_rows = out_0.rearrange("(p t) m -> p t m", t=PACK)
+
+        def look_first(t, engine_copy):
+            engine_copy(firsts[t][:], wide[t][:].indirect(first_list[:]))
+
+        def look_second(t, engine_copy):
+            engine_copy(seconds[t][:], wide[t][:].indirect(second_list[:]))
+
+        def look_second_times_first(t):
+            nc.vector.tensor_tensor(seconds[t][:], wide[t][:].indirect(second_list[:]), firsts[t][:], MULT)
+
+        def place_product_on_vector(t):
+            nc.vector.tensor_tensor(placed[t][:].indirect(place_list[:]), firsts[t][:], seconds[t][:], MULT)
+
+        def place_on_scalar(t):
+            for part in range(2):
+                nc.scalar.activation(
+                    placed[t][:].indirect(place_list[:, 16 * part : 16 * (part + 1)]),
+                    seconds[t][:, 256 * part : 256 * (part + 1)],
+                    COPY,
+                )
+
+        def add_old(t):
+            for h in range(2):
+                cols = slice(h * HALF, (h + 1) * HALF)
+                nc.vector.scalar_tensor_tensor(
+                    result[h][:, t, :], olds[t][:, cols], fades[:, t : t + 1], placed[t][:, cols], MULT, ADD
+                )
+                nc.sync.dma_start(out_rows[:, t, cols], result[h][:, t, :])
+
+        leave_bank(0, 0, on_scalar)
+        leave_bank(1, 0, on_vector)
+        leave_bank(0, 1, on_vector)
+        leave_bank(1, 1, on_scalar)
+        look_first(0, on_vector)
+        look_second(0, on_scalar)
+        place_product_on_vector(0)
+        look_first(1, on_scalar)
+        look_second_times_first(1)
+        leave_bank(2, 0, on_scalar)
+        leave_bank(2, 1, on_scalar)
+        look_first(2, on_scalar)
+        look_second(2, on_scalar)
+        place_product_on_vector(2)
+        leave_bank(3, 0, on_scalar)
+        leave_bank(3, 1, on_scalar)
+        look_first(3, on_scalar)
+        place_on_scalar(1)
+        look_second_times_first(3)
+        place_on_scalar(3)
+        add_old(0)
+        add_old(2)
+        add_old(1)
+        add_old(3)
+
+        out_codes = [tile([P, HALF], U32, "out_codes%d" % h) for h in range(2)]
+        out_scales = tile([P, M], U8, "out_scales")
+        words_out = out_1[0].rearrange("p c t -> p (c t)").bitcast(I32)
+        for c in range(M // CHUNK):
+            h = c // 2
+            cols = slice((c % 2) * CHUNK, (c % 2 + 1) * CHUNK)
+            rounded = tile([P, CHUNK, PACK], BF16, "rounded%d" % c)
+            interleave(on_scalar if c % 2 == 0 else on_vector, rounded[:], result[h][:, :, cols])
+            nc.vector.quantize_mx(
+                out=out_codes[h][:, cols].bitcast(FP8X4),
+                scales=out_scales[:, c * CHUNK : (c + 1) * CHUNK],
+                in_=rounded[:].rearrange("p c t -> p (c t)"),
+            )
+            if c % 2 == 1:
+                nc.sync.dma_start(words_out[:, h * HALF : (h + 1) * HALF], out_codes[h][:].bitcast(I32))
+        for q in range(4):
+            queue = nc.scalar if q % 2 == 0 else nc.sync
+            queue.dma_start(
+                out_2[0, 4 * q : 4 * q + 4, :].bitcast(I32),
+                out_scales[32 * q : 32 * q + 4, :].bitcast(I32),
+            )

@@ -45,13 +45,15 @@ def tile_attend_tab_lookedtimes_keep_pl_kernel(
     with ExitStack() as ctx:
         lists = ctx.enter_context(tc.tile_pool(name="lists", bufs=1))
         keep = ctx.enter_context(tc.tile_pool(name="keep", bufs=1))
+        relay = ctx.enter_context(tc.tile_pool(name="relay", bufs=1))
         psum = ctx.enter_context(tc.psum_pool(name="psum", bufs=1))
 
         def tile(shape, dtype, name):
             return keep.tile(shape, dtype, name=name, align_bytes=64)
 
-        pool_scales = tile([P, T], U8, "pool_scales")
-        nc.gpsimd.memset(pool_scales[:].bitcast(I32), 0)
+        pool_scales = relay.tile([P, T], U8, name="pool_scales", offset=0, align_bytes=64)
+        nc.vector.memset(pool_scales[:, : T // 2].bitcast(I32), 0)
+        nc.gpsimd.memset(pool_scales[:, T // 2 :].bitcast(I32), 0)
 
         pool_words = tile([P, T], U16, "pool_words")
         nc.sync.dma_start(pool_words[:].bitcast(I32), keys_words[0].bitcast(I32))
@@ -85,56 +87,77 @@ def tile_attend_tab_lookedtimes_keep_pl_kernel(
 
         placed = [tile([P, M], F32, "placed%d" % t) for t in range(PACK)]
         for t in range(PACK):
-            nc.vector.memset(placed[t][:], 0.0)
+            nc.gpsimd.memset(placed[t][:], 0.0)
 
         picked_words = tile([P, I], U16, "picked_words")
         nc.vector.tensor_copy(picked_words[:], pool_words[:].indirect(token_list[:]))
-        key_words = tile([P, PACK, P], U16, "key_words")
-        nc.vector.tensor_copy(key_words[:], picked_words[:].rearrange("p (s t) -> p t s", t=PACK))
         key_scales = tile([P, PACK, P], U8, "key_scales")
         nc.vector.tensor_copy(key_scales[:].rearrange("p t s -> p s t"), pool_scales[:].indirect(token_list[:]))
+        key_words = relay.tile([P, PACK, P], U16, name="key_words", offset=0, align_bytes=64)
+        nc.vector.tensor_copy(key_words[:], picked_words[:].rearrange("p (s t) -> p t s", t=PACK))
 
-        note_codes = [tile([P, HALF], U32, "note_codes%d" % h) for h in range(2)]
-        note_scales = [tile([P, HALF], U8, "note_scales%d" % h) for h in range(2)]
-        wide = [tile([P, U], F32, "wide%d" % t) for t in range(PACK)]
-        banks = {}
+        note_codes = [
+            relay.tile([P, CHUNK], U32, name="note_codes0", offset=T // 2, align_bytes=64),
+            keep.tile([P, CHUNK], U32, name="note_codes1", tag="notes_raw2", align_bytes=64),
+            tile([P, CHUNK], U32, "note_codes2"),
+            tile([P, CHUNK], U32, "note_codes3"),
+        ]
+        note_scales = [tile([P, CHUNK], U8, "note_scales%d" % c) for c in range(4)]
+        wide = [
+            keep.tile([P, U], F32, name="wide%d" % t, tag="shared0" if t == 3 else "wide%d" % t, align_bytes=64)
+            for t in range(PACK)
+        ]
+        grouped = {}
 
-        def quantise_notes(c, engine_copy):
-            grouped = tile([P, CHUNK, PACK], BF16, "notes_grouped%d" % (c % 2))
-            interleave(engine_copy, grouped[:], notes_raw[c][:])
-            cols = slice((c % 2) * CHUNK, (c % 2 + 1) * CHUNK)
+        def round_notes(c, engine_copy):
+            grouped[c] = tile([P, CHUNK, PACK], BF16, "notes_grouped%d" % (c % 2))
+            interleave(engine_copy, grouped[c][:], notes_raw[c][:])
+
+        def quantise_notes(c):
             nc.vector.quantize_mx(
-                out=note_codes[c // 2][:, cols].bitcast(FP8X4),
-                scales=note_scales[c // 2][:, cols],
-                in_=grouped[:].rearrange("p c t -> p (c t)"),
+                out=note_codes[c][:].bitcast(FP8X4),
+                scales=note_scales[c][:],
+                in_=grouped[c][:].rearrange("p c t -> p (c t)"),
             )
 
-        def multiply(h):
-            for t in range(PACK):
-                banks[t, h] = psum.tile([P, HALF], F32, name="bank%d_%d" % (t, h))
+        def multiply(t, chunks, bank_number, engine_copy):
+            bank = psum.tile([P, len(chunks), CHUNK], F32, name="bank%d" % bank_number)
+            for place, c in reversed(list(enumerate(chunks))):
                 nc.tensor.matmul_mx(
-                    out=banks[t, h][:],
+                    out=bank[:, place, :],
                     lhsT=key_words[:, t, :].bitcast(U8).bitcast(FP4X4),
                     lhsT_scale=key_scales[:, t, :],
-                    rhs=note_codes[h][:].bitcast(FP8X4),
-                    rhs_scale=note_scales[h][:],
+                    rhs=note_codes[c][:].bitcast(FP8X4),
+                    rhs_scale=note_scales[c][:],
                     start=True,
                     stop=True,
                 )
+            by_chunk = wide[t][:].rearrange("p (c u) -> p c u", u=CHUNK)
+            step = chunks[-1] - chunks[0] if len(chunks) > 1 else 1
+            engine_copy(by_chunk[:, chunks[0] : chunks[-1] + 1 : step, :], bank[:])
 
-        def leave_bank(t, h, engine_copy):
-            engine_copy(wide[t][:, h * HALF : (h + 1) * HALF], banks[t, h][:])
+        round_notes(0, on_scalar)
+        round_notes(1, on_scalar)
+        quantise_notes(0)
+        round_notes(2, on_vector)
+        quantise_notes(1)
+        quantise_notes(2)
+        round_notes(3, on_vector)
+        quantise_notes(3)
+        for t in range(PACK):
+            multiply(t, [0], t, on_scalar)
+        multiply(0, [1], 4, on_scalar)
+        multiply(1, [1], 5, on_scalar)
+        multiply(0, [2], 6, on_scalar)
+        multiply(0, [3], 1, on_vector)
+        multiply(2, [1], 7, on_scalar)
+        multiply(3, [1], 0, on_scalar)
 
-        quantise_notes(0, on_scalar)
-        quantise_notes(1, on_scalar)
-        multiply(0)
-        quantise_notes(2, on_scalar)
-        quantise_notes(3, on_vector)
-        multiply(1)
-
-        firsts = [tile([P, J], F32, "first%d" % t) for t in range(PACK)]
+        firsts = [
+            keep.tile([P, J], F32, name="first%d" % t, tag="shared1" if t == 3 else "first%d" % t, align_bytes=64)
+            for t in range(PACK)
+        ]
         seconds = [tile([P, J], F32, "second%d" % t) for t in range(PACK)]
-        result = [tile([P, PACK, HALF], F32, "result%d" % h) for h in range(2)]
         out_rows = out_0.rearrange("(p t) m -> p t m", t=PACK)
 
         def look_first(t, engine_copy):
@@ -157,54 +180,72 @@ def tile_attend_tab_lookedtimes_keep_pl_kernel(
                     COPY,
                 )
 
-        def add_old(t):
-            for h in range(2):
-                cols = slice(h * HALF, (h + 1) * HALF)
-                nc.vector.scalar_tensor_tensor(
-                    result[h][:, t, :], olds[t][:, cols], fades[:, t : t + 1], placed[t][:, cols], MULT, ADD
-                )
-                nc.sync.dma_start(out_rows[:, t, cols], result[h][:, t, :])
-
-        leave_bank(0, 0, on_scalar)
-        leave_bank(1, 0, on_vector)
-        leave_bank(0, 1, on_vector)
-        leave_bank(1, 1, on_scalar)
         look_first(0, on_vector)
         look_second(0, on_scalar)
+        multiply(1, [2, 3], 2, on_vector)
         place_product_on_vector(0)
+        multiply(2, [2, 3], 3, on_scalar)
         look_first(1, on_scalar)
         look_second_times_first(1)
-        leave_bank(2, 0, on_scalar)
-        leave_bank(2, 1, on_scalar)
         look_first(2, on_scalar)
         look_second(2, on_scalar)
         place_product_on_vector(2)
-        leave_bank(3, 0, on_scalar)
-        leave_bank(3, 1, on_scalar)
+        multiply(3, [2, 3], 4, on_scalar)
         look_first(3, on_scalar)
         place_on_scalar(1)
         look_second_times_first(3)
         place_on_scalar(3)
-        add_old(0)
-        add_old(2)
-        add_old(1)
-        add_old(3)
 
-        out_codes = [tile([P, HALF], U32, "out_codes%d" % h) for h in range(2)]
+        result = [
+            keep.tile([P, PACK, HALF], F32, name="result%d" % h, tag="shared%d" % h, align_bytes=64) for h in range(2)
+        ]
+
+        def add_old(t, width):
+            for start in range(0, M, width):
+                h, within = divmod(start, HALF)
+                cols = slice(start, start + width)
+                nc.vector.scalar_tensor_tensor(
+                    result[h][:, t, within : within + width],
+                    olds[t][:, cols],
+                    fades[:, t : t + 1],
+                    placed[t][:, cols],
+                    MULT,
+                    ADD,
+                )
+                if within + width == HALF:
+                    nc.sync.dma_start(out_rows[:, t, h * HALF : (h + 1) * HALF], result[h][:, t, :])
+
+        add_old(0, HALF)
+        add_old(2, HALF)
+        add_old(1, HALF)
+        add_old(3, CHUNK)
+
         out_scales = tile([P, M], U8, "out_scales")
         words_out = out_1[0].rearrange("p c t -> p (c t)").bitcast(I32)
-        for c in range(M // CHUNK):
-            h = c // 2
-            cols = slice((c % 2) * CHUNK, (c % 2 + 1) * CHUNK)
-            rounded = tile([P, CHUNK, PACK], BF16, "rounded%d" % c)
-            interleave(on_scalar if c % 2 == 0 else on_vector, rounded[:], result[h][:, :, cols])
+        rounded = {}
+
+        def round_result(start, stop, engine_copy):
+            h, within = divmod(start, HALF)
+            rounded[start] = tile([P, stop - start, PACK], BF16, "rounded%d" % start)
+            interleave(engine_copy, rounded[start][:], result[h][:, :, within : within + stop - start])
+
+        def quantise_result(start, stop):
+            codes = tile([P, stop - start], U32, "out_codes%d" % start)
             nc.vector.quantize_mx(
-                out=out_codes[h][:, cols].bitcast(FP8X4),
-                scales=out_scales[:, c * CHUNK : (c + 1) * CHUNK],
-                in_=rounded[:].rearrange("p c t -> p (c t)"),
+                out=codes[:].bitcast(FP8X4),
+                scales=out_scales[:, start:stop],
+                in_=rounded[start][:].rearrange("p c t -> p (c t)"),
             )
-            if c % 2 == 1:
-                nc.sync.dma_start(words_out[:, h * HALF : (h + 1) * HALF], out_codes[h][:].bitcast(I32))
+            nc.sync.dma_start(words_out[:, start:stop], codes[:].bitcast(I32))
+
+        round_result(0, 256, on_scalar)
+        round_result(256, 512, on_scalar)
+        round_result(512, 640, on_scalar)
+        round_result(640, 1024, on_vector)
+        quantise_result(0, 256)
+        quantise_result(640, 1024)
+        quantise_result(256, 512)
+        quantise_result(512, 640)
         for q in range(4):
             queue = nc.scalar if q % 2 == 0 else nc.sync
             queue.dma_start(

@@ -52,8 +52,7 @@ def tile_attend_tab_lookedtimes_keep_pl_kernel(
             return keep.tile(shape, dtype, name=name, align_bytes=64)
 
         pool_scales = relay.tile([P, T], U8, name="pool_scales", offset=0, align_bytes=64)
-        nc.vector.memset(pool_scales[:, : T // 2].bitcast(I32), 0)
-        nc.gpsimd.memset(pool_scales[:, T // 2 :].bitcast(I32), 0)
+        nc.vector.memset(pool_scales[:].bitcast(I32), 0)
 
         pool_words = tile([P, T], U16, "pool_words")
         nc.sync.dma_start(pool_words[:].bitcast(I32), keys_words[0].bitcast(I32))
@@ -87,7 +86,7 @@ def tile_attend_tab_lookedtimes_keep_pl_kernel(
 
         placed = [tile([P, M], F32, "placed%d" % t) for t in range(PACK)]
         for t in range(PACK):
-            nc.gpsimd.memset(placed[t][:], 0.0)
+            nc.vector.memset(placed[t][:].bitcast(I32), 0)
 
         picked_words = tile([P, I], U16, "picked_words")
         nc.vector.tensor_copy(picked_words[:], pool_words[:].indirect(token_list[:]))

@@ -151,9 +151,10 @@ def tile_attend_tab_lookedtimes_keep_pl_kernel(
         multiply(0, [3], 1, on_vector)
         multiply(2, [1], 7, on_scalar)
         multiply(3, [1], 0, on_scalar)
+        multiply(1, [2], 2, on_scalar)
 
         firsts = [
-            keep.tile([P, J], F32, name="first%d" % t, tag="shared1" if t == 3 else "first%d" % t, align_bytes=64)
+            keep.tile([P, J], F32, name="first%d" % t, tag="shared1" if t == 1 else "first%d" % t, align_bytes=64)
             for t in range(PACK)
         ]
         seconds = [tile([P, J], F32, "second%d" % t) for t in range(PACK)]
@@ -171,53 +172,62 @@ def tile_attend_tab_lookedtimes_keep_pl_kernel(
         def place_product_on_vector(t):
             nc.vector.tensor_tensor(placed[t][:].indirect(place_list[:]), firsts[t][:], seconds[t][:], MULT)
 
-        def place_on_scalar(t):
-            for part in range(2):
-                nc.scalar.activation(
-                    placed[t][:].indirect(place_list[:, 16 * part : 16 * (part + 1)]),
-                    seconds[t][:, 256 * part : 256 * (part + 1)],
-                    COPY,
-                )
+        def place_on_scalar(t, part):
+            nc.scalar.activation(
+                placed[t][:].indirect(place_list[:, 16 * part : 16 * (part + 1)]),
+                seconds[t][:, 256 * part : 256 * (part + 1)],
+                COPY,
+            )
 
         look_first(0, on_vector)
         look_second(0, on_scalar)
-        multiply(1, [2, 3], 2, on_vector)
+        multiply(1, [3], 5, on_vector)
         place_product_on_vector(0)
+        multiply(3, [2, 3], 4, on_scalar)
         multiply(2, [2, 3], 3, on_scalar)
         look_first(1, on_scalar)
+        look_first(3, on_scalar)
         look_second_times_first(1)
+        look_second_times_first(3)
         look_first(2, on_scalar)
         look_second(2, on_scalar)
-        place_product_on_vector(2)
-        multiply(3, [2, 3], 4, on_scalar)
-        look_first(3, on_scalar)
-        place_on_scalar(1)
-        look_second_times_first(3)
-        place_on_scalar(3)
 
         result = [
             keep.tile([P, PACK, HALF], F32, name="result%d" % h, tag="shared%d" % h, align_bytes=64) for h in range(2)
         ]
 
-        def add_old(t, width):
-            for start in range(0, M, width):
-                h, within = divmod(start, HALF)
-                cols = slice(start, start + width)
-                nc.vector.scalar_tensor_tensor(
-                    result[h][:, t, within : within + width],
-                    olds[t][:, cols],
-                    fades[:, t : t + 1],
-                    placed[t][:, cols],
-                    MULT,
-                    ADD,
-                )
-                if within + width == HALF:
-                    nc.sync.dma_start(out_rows[:, t, h * HALF : (h + 1) * HALF], result[h][:, t, :])
+        def add_old(t, start, stop):
+            h, within = divmod(start, HALF)
+            nc.vector.scalar_tensor_tensor(
+                result[h][:, t, within : within + stop - start],
+                olds[t][:, start:stop],
+                fades[:, t : t + 1],
+                placed[t][:, start:stop],
+                MULT,
+                ADD,
+            )
 
-        add_old(0, HALF)
-        add_old(2, HALF)
-        add_old(1, HALF)
-        add_old(3, CHUNK)
+        def store_half(t, h):
+            nc.sync.dma_start(out_rows[:, t, h * HALF : (h + 1) * HALF], result[h][:, t, :])
+
+        def add_old_by_halves(t):
+            for h in range(2):
+                add_old(t, h * HALF, (h + 1) * HALF)
+                store_half(t, h)
+
+        place_product_on_vector(2)
+        for part in range(2):
+            place_on_scalar(1, part)
+            place_on_scalar(3, part)
+        add_old_by_halves(0)
+        add_old_by_halves(2)
+        add_old_by_halves(1)
+        add_old(3, 0, 256)
+        add_old(3, 512, 768)
+        add_old(3, 768, 1024)
+        store_half(3, 1)
+        add_old(3, 256, 512)
+        store_half(3, 0)
 
         out_scales = tile([P, M], U8, "out_scales")
         words_out = out_1[0].rearrange("p c t -> p (c t)").bitcast(I32)

@@ -22,6 +22,7 @@ PACK = 4
 CHUNK = 256
 HALF = 512
 LIST_COLS = J // 16
+SCATTER_PART = 256
 
 
 def interleave(engine_copy, dst, src):
@@ -132,8 +133,7 @@ def tile_attend_tab_lookedtimes_keep_pl_kernel(
                     stop=True,
                 )
             by_chunk = wide[t][:].rearrange("p (c u) -> p c u", u=CHUNK)
-            step = chunks[-1] - chunks[0] if len(chunks) > 1 else 1
-            engine_copy(by_chunk[:, chunks[0] : chunks[-1] + 1 : step, :], bank[:])
+            engine_copy(by_chunk[:, chunks[0] : chunks[-1] + 1, :], bank[:])
 
         round_notes(0, on_scalar)
         round_notes(1, on_scalar)
@@ -174,14 +174,14 @@ def tile_attend_tab_lookedtimes_keep_pl_kernel(
 
         def place_on_scalar(t, part):
             nc.scalar.activation(
-                placed[t][:].indirect(place_list[:, 16 * part : 16 * (part + 1)]),
-                seconds[t][:, 256 * part : 256 * (part + 1)],
+                placed[t][:].indirect(place_list[:, part * SCATTER_PART // 16 : (part + 1) * SCATTER_PART // 16]),
+                seconds[t][:, part * SCATTER_PART : (part + 1) * SCATTER_PART],
                 COPY,
             )
 
         look_first(0, on_vector)
         look_second(0, on_scalar)
-        multiply(1, [3], 5, on_vector)
+        multiply(1, [3], 5, on_scalar)
         place_product_on_vector(0)
         multiply(3, [2, 3], 4, on_scalar)
         multiply(2, [2, 3], 3, on_scalar)
@@ -215,11 +215,11 @@ def tile_attend_tab_lookedtimes_keep_pl_kernel(
                 add_old(t, h * HALF, (h + 1) * HALF)
                 store_half(t, h)
 
+        add_old_by_halves(0)
         place_product_on_vector(2)
-        for part in range(2):
+        for part in range(J // SCATTER_PART):
             place_on_scalar(1, part)
             place_on_scalar(3, part)
-        add_old_by_halves(0)
         add_old_by_halves(2)
         add_old_by_halves(1)
         add_old(3, 0, 256)

from contextlib import ExitStack

import concourse.mybir as mybir

D, T, I, J, U, M = 512, 2048, 512, 512, 1024, 1024
FLOPS = 2 * D * I * U

F32 = mybir.dt.float32
BF16 = mybir.dt.bfloat16
I32 = mybir.dt.int32
U32 = mybir.dt.uint32
U16 = mybir.dt.uint16
U8 = mybir.dt.uint8
FP8X4 = mybir.dt.float8_e4m3fn_x4
FP4X4 = mybir.dt.float4_e2m1fn_x4
MULT = mybir.AluOpType.mult
ADD = mybir.AluOpType.add
COPY = mybir.ActivationFunctionType.Copy

P = 128
PACK = 4
CHUNK = 256
HALF = 512
LIST_COLS = J // 16
SCATTER_PART = 256


def interleave(engine_copy, dst, src):
    engine_copy(
        dst.rearrange("p (c i) t -> p c t i", i=4),
        src.rearrange("p t (c i) -> p c t i", i=4),
    )


def tile_attend_tab_lookedtimes_keep_pl_kernel(
    tc, keys_words, keys_scales, notes, old, fade, offs, offs2, offs3, offs4, out_0, out_1, out_2
):
    nc = tc.nc

    def on_vector(dst, src):
        nc.vector.tensor_copy(dst, src)

    def on_scalar(dst, src):
        nc.scalar.activation(dst, src, COPY)

    with ExitStack() as ctx:
        lists = ctx.enter_context(tc.tile_pool(name="lists", bufs=1))
        keep = ctx.enter_context(tc.tile_pool(name="keep", bufs=1))
        relay = ctx.enter_context(tc.tile_pool(name="relay", bufs=1))
        psum = ctx.enter_context(tc.psum_pool(name="psum", bufs=1))

        def tile(shape, dtype, name):
            return keep.tile(shape, dtype, name=name, align_bytes=64)

        pool_scales = relay.tile([P, T], U8, name="pool_scales", offset=0, align_bytes=64)
        nc.vector.memset(pool_scales[:].bitcast(I32), 0)

        pool_words = tile([P, T], U16, "pool_words")
        nc.sync.dma_start(pool_words[:].bitcast(I32), keys_words[0].bitcast(I32))
        token_list = lists.tile([P, LIST_COLS], U16, name="token_list")
        nc.sync.dma_start(token_list[:], offs)
        for q in range(4):
            nc.sync.dma_start(
                pool_scales[32 * q : 32 * q + 4, :].bitcast(I32),
                keys_scales[0, 4 * q : 4 * q + 4, :].bitcast(I32),
            )
        notes_rows = notes.rearrange("(p t) u -> p t u", t=PACK)
        notes_raw = []
        for c in range(U // CHUNK):
            raw = tile([P, PACK, CHUNK], F32, "notes_raw%d" % c)
            nc.sync.dma_start(raw[:], notes_rows[:, :, c * CHUNK : (c + 1) * CHUNK])
            notes_raw.append(raw)
        first_list = lists.tile([P, LIST_COLS], U16, name="first_list")
        nc.sync.dma_start(first_list[:], offs2)
        second_list = lists.tile([P, LIST_COLS], U16, name="second_list")
        nc.sync.dma_start(second_list[:], offs3)
        place_list = lists.tile([P, LIST_COLS], U16, name="place_list")
        nc.sync.dma_start(place_list[:], offs4)
        fades = tile([P, PACK], F32, "fades")
        nc.sync.dma_start(fades[:], fade.rearrange("(p t) one -> p (t one)", t=PACK))
        old_rows = old.rearrange("(p t) m -> p t m", t=PACK)
        olds = []
        for t in range(PACK):
            before = tile([P, M], F32, "old%d" % t)
            nc.sync.dma_start(before[:], old_rows[:, t, :])
            olds.append(before)

        placed = [tile([P, M], F32, "placed%d" % t) for t in range(PACK)]
        for t in range(PACK):
            nc.vector.memset(placed[t][:].bitcast(I32), 0)

        picked_words = tile([P, I], U16, "picked_words")
        nc.vector.tensor_copy(picked_words[:], pool_words[:].indirect(token_list[:]))
        key_scales = tile([P, PACK, P], U8, "key_scales")
        nc.vector.tensor_copy(key_scales[:].rearrange("p t s -> p s t"), pool_scales[:].indirect(token_list[:]))
        key_words = relay.tile([P, PACK, P], U16, name="key_words", offset=0, align_bytes=64)
        nc.vector.tensor_copy(key_words[:], picked_words[:].rearrange("p (s t) -> p t s", t=PACK))

        note_codes = [
            relay.tile([P, CHUNK], U32, name="note_codes0", offset=T // 2, align_bytes=64),
            keep.tile([P, CHUNK], U32, name="note_codes1", tag="notes_raw2", align_bytes=64),
            tile([P, CHUNK], U32, "note_codes2"),
            tile([P, CHUNK], U32, "note_codes3"),
        ]
        note_scales = [tile([P, CHUNK], U8, "note_scales%d" % c) for c in range(4)]
        wide = [
            keep.tile([P, U], F32, name="wide%d" % t, tag="shared0" if t == 3 else "wide%d" % t, align_bytes=64)
            for t in range(PACK)
        ]
        grouped = {}

        def round_notes(c, engine_copy):
            grouped[c] = tile([P, CHUNK, PACK], BF16, "notes_grouped%d" % (c % 2))
            interleave(engine_copy, grouped[c][:], notes_raw[c][:])

        def quantise_notes(c):
            nc.vector.quantize_mx(
                out=note_codes[c][:].bitcast(FP8X4),
                scales=note_scales[c][:],
                in_=grouped[c][:].rearrange("p c t -> p (c t)"),
            )

        def multiply(t, chunks, bank_number, engine_copy):
            bank = psum.tile([P, len(chunks), CHUNK], F32, name="bank%d" % bank_number)
            for place, c in reversed(list(enumerate(chunks))):
                nc.tensor.matmul_mx(
                    out=bank[:, place, :],
                    lhsT=key_words[:, t, :].bitcast(U8).bitcast(FP4X4),
                    lhsT_scale=key_scales[:, t, :],
                    rhs=note_codes[c][:].bitcast(FP8X4),
                    rhs_scale=note_scales[c][:],
                    start=True,
                    stop=True,
                )
            by_chunk = wide[t][:].rearrange("p (c u) -> p c u", u=CHUNK)
            engine_copy(by_chunk[:, chunks[0] : chunks[-1] + 1, :], bank[:])

        round_notes(0, on_scalar)
        round_notes(1, on_scalar)
        quantise_notes(0)
        round_notes(2, on_vector)
        quantise_notes(1)
        quantise_notes(2)
        round_notes(3, on_vector)
        quantise_notes(3)
        for t in range(PACK):
            multiply(t, [0], t, on_scalar)
        multiply(0, [1], 4, on_scalar)
        multiply(1, [1], 5, on_scalar)
        multiply(0, [2], 6, on_scalar)
        multiply(0, [3], 1, on_vector)
        multiply(2, [1], 7, on_scalar)
        multiply(3, [1], 0, on_scalar)
        multiply(1, [2], 2, on_scalar)

        firsts = [
            keep.tile([P, J], F32, name="first%d" % t, tag="shared1" if t == 1 else "first%d" % t, align_bytes=64)
            for t in range(PACK)
        ]
        seconds = [tile([P, J], F32, "second%d" % t) for t in range(PACK)]
        out_rows = out_0.rearrange("(p t) m -> p t m", t=PACK)

        def look_first(t, engine_copy):
            engine_copy(firsts[t][:], wide[t][:].indirect(first_list[:]))

        def look_second(t, engine_copy):
            engine_copy(seconds[t][:], wide[t][:].indirect(second_list[:]))

        def look_second_times_first(t):
            nc.vector.tensor_tensor(seconds[t][:], wide[t][:].indirect(second_list[:]), firsts[t][:], MULT)

        def place_product_on_vector(t):
            nc.vector.tensor_tensor(placed[t][:].indirect(place_list[:]), firsts[t][:], seconds[t][:], MULT)

        def place_on_scalar(t, part):
            nc.scalar.activation(
                placed[t][:].indirect(place_list[:, part * SCATTER_PART // 16 : (part + 1) * SCATTER_PART // 16]),
                seconds[t][:, part * SCATTER_PART : (part + 1) * SCATTER_PART],
                COPY,
            )

        look_first(0, on_vector)
        look_second(0, on_scalar)
        multiply(1, [3], 5, on_scalar)
        place_product_on_vector(0)
        multiply(3, [2, 3], 4, on_scalar)
        multiply(2, [2, 3], 3, on_scalar)
        look_first(1, on_scalar)
        look_first(3, on_scalar)
        look_second_times_first(1)
        look_second_times_first(3)
        look_first(2, on_scalar)
        look_second(2, on_scalar)

        result = [
            keep.tile([P, PACK, HALF], F32, name="result%d" % h, tag="shared%d" % h, align_bytes=64) for h in range(2)
        ]

        def add_old(t, start, stop):
            h, within = divmod(start, HALF)
            nc.vector.scalar_tensor_tensor(
                result[h][:, t, within : within + stop - start],
                olds[t][:, start:stop],
                fades[:, t : t + 1],
                placed[t][:, start:stop],
                MULT,
                ADD,
            )

        def store_half(t, h):
            nc.sync.dma_start(out_rows[:, t, h * HALF : (h + 1) * HALF], result[h][:, t, :])

        def add_old_by_halves(t):
            for h in range(2):
                add_old(t, h * HALF, (h + 1) * HALF)
                store_half(t, h)

        add_old_by_halves(0)
        place_product_on_vector(2)
        for part in range(J // SCATTER_PART):
            place_on_scalar(1, part)
            place_on_scalar(3, part)
        add_old_by_halves(2)
        add_old_by_halves(1)
        add_old(3, 0, 256)
        add_old(3, 512, 768)
        add_old(3, 768, 1024)
        store_half(3, 1)
        add_old(3, 256, 512)
        store_half(3, 0)

        out_scales = tile([P, M], U8, "out_scales")
        words_out = out_1[0].rearrange("p c t -> p (c t)").bitcast(I32)
        rounded = {}

        def round_result(start, stop, engine_copy):
            h, within = divmod(start, HALF)
            rounded[start] = tile([P, stop - start, PACK], BF16, "rounded%d" % start)
            interleave(engine_copy, rounded[start][:], result[h][:, :, within : within + stop - start])

        def quantise_result(start, stop):
            codes = tile([P, stop - start], U32, "out_codes%d" % start)
            nc.vector.quantize_mx(
                out=codes[:].bitcast(FP8X4),
                scales=out_scales[:, start:stop],
                in_=rounded[start][:].rearrange("p c t -> p (c t)"),
            )
            nc.sync.dma_start(words_out[:, start:stop], codes[:].bitcast(I32))

        round_result(0, 256, on_scalar)
        round_result(256, 512, on_scalar)
        round_result(512, 640, on_scalar)
        round_result(640, 1024, on_vector)
        quantise_result(0, 256)
        quantise_result(640, 1024)
        quantise_result(256, 512)
        quantise_result(512, 640)
        for q in range(4):
            queue = nc.scalar if q % 2 == 0 else nc.sync
            queue.dma_start(
                out_2[0, 4 * q : 4 * q + 4, :].bitcast(I32),
                out_scales[32 * q : 32 * q + 4, :].bitcast(I32),
            )
